import numpy as np
import ml_dtypes


def mxq(x, axis, fmt="e4m3"):
    dtype, down = {"e4m3": (ml_dtypes.float8_e4m3fn, 7), "e5m2": (ml_dtypes.float8_e5m2, 14)}[fmt]
    v = np.moveaxis(np.asarray(x, np.float32).astype(ml_dtypes.bfloat16).astype(np.float64), axis, -1)
    blocks = v.reshape(v.shape[:-1] + (-1, 32))
    amax = np.abs(blocks).max(-1, keepdims=True)
    byte = np.maximum(np.where(amax > 0, np.frexp(amax)[1] - 1 + 127, 0) - down, 1)
    scale = np.exp2(byte - 127.0)
    codes = (blocks / scale).astype(np.float32).astype(dtype).astype(np.float64)
    return np.moveaxis((codes * scale).reshape(v.shape), -1, axis)


WIDE = False


def mx_kscale(k):
    if not WIDE:
        return np.ones(k)
    levels = np.array([10, -10, 5, -5, 0])
    if k % 512:
        return np.exp2(np.random.permutation(np.resize(levels, k // 32))).repeat(32)
    a = np.empty((k // 512, 16))
    for p in range(k // 512):
        a[p, :8] = np.random.permutation(np.resize(levels, 8))
        for g in range(8):
            far = levels[np.abs(levels - a[p, g]) >= 10]
            a[p, g + 8] = far[np.random.randint(len(far))]
    return np.exp2(a.ravel()).repeat(32)


def f64(x):
    return np.asarray(x).astype(np.float64)


def striped8(idx):
    return np.asarray(idx).reshape(8, -1, 16).transpose(0, 2, 1).reshape(128, -1).astype(np.uint16)


def unstriped8(offs):
    return offs.reshape(8, 16, -1).transpose(0, 2, 1).reshape(8, -1).astype(np.int64)


def pick8(x, idx, run):
    r = np.arange(len(x))
    return x[r[:, None], idx[r % (8 * run) // run]]


E2M1 = np.array([0.0, 0.5, 1.0, 1.5, 2.0, 3.0, 4.0, 6.0, -0.0, -0.5, -1.0, -1.5, -2.0, -3.0, -4.0, -6.0])


def pack_weight(w, fmt):
    k, n = w.shape
    w = f64(np.asarray(w, np.float32).astype(ml_dtypes.bfloat16)).reshape(k // 32, 32, n)
    amax = np.abs(w).max(1)
    if fmt == "e4m3":
        byte = np.frexp(amax)[1] - 1 + 127 - 7
    else:
        mant, ex = np.frexp(amax / 6.0)
        byte = np.where(mant > 0.5, ex, ex - 1) + 127
    byte = np.clip(np.where(amax > 0, byte, 1), 1, 254)
    scaled = (w * np.exp2(127.0 - byte)[:, None, :]).reshape(k, n).astype(np.float32)
    by_word = np.ascontiguousarray(scaled.reshape(k // 512, 128, 4, n).transpose(0, 1, 3, 2))
    if fmt == "e4m3":
        words = by_word.astype(ml_dtypes.float8_e4m3fn).view(np.uint8)
    else:
        c = by_word.astype(ml_dtypes.float4_e2m1fn).view(np.uint8) & 0xF
        words = (c[..., 0::2] | (c[..., 1::2] << 4)).reshape(k // 512, 128, 2 * n)
    return np.ascontiguousarray(words), np.ascontiguousarray(byte.astype(np.uint8).reshape(k // 512, 16, n))


def unpack_weight(words, scales, fmt):
    g, _, n = scales.shape
    words = np.ascontiguousarray(words).reshape(g, 128, n, -1)
    if fmt == "e4m3":
        vals = words.view(ml_dtypes.float8_e4m3fn).astype(np.float64)
    else:
        nib = np.empty((g, 128, n, 4), np.uint8)
        nib[..., 0::2] = words & 0xF
        nib[..., 1::2] = words >> 4
        vals = E2M1[nib]
    vals = vals * np.repeat(np.exp2(scales.astype(np.float64) - 127.0), 8, axis=1)[..., None]
    return vals.transpose(0, 1, 3, 2).reshape(g * 512, n)


D, T, U, X, S, I, J, Q = 512, 1024, 1024, 1024, 1024, 512, 256, 128


def setup_inputs():
    n = np.random.standard_normal
    idx = np.stack([np.random.permutation(T)[:I] for _ in range(8)])
    idx2 = np.stack([np.random.permutation(U)[:I] for _ in range(8)])
    idx3 = np.stack([np.random.permutation(X)[:J] for _ in range(8)])
    idx4 = np.stack([np.random.permutation(S)[:J] for _ in range(8)])
    idx5 = np.stack([np.random.permutation(S)[:I] for _ in range(8)])
    fd = mx_kscale(D)
    keysp = pack_weight(n((D, T)) / fd[:, None], "e4m3")
    notesp = pack_weight(n((D, U)) / fd[:, None], "e2m1")
    usersp = pack_weight(n((D, X)) / fd[:, None], "e4m3")
    shelvesp = pack_weight(n((D, S)) / fd[:, None], "e2m1")
    return {
        "query": (n((D, Q)) * 1.0 / np.sqrt(D) * fd[:, None]).astype(np.float32),
        "keys_words": keysp[0],
        "keys_scales": keysp[1],
        "notes_words": notesp[0],
        "notes_scales": notesp[1],
        "users_words": usersp[0],
        "users_scales": usersp[1],
        "shelves_words": shelvesp[0],
        "shelves_scales": shelvesp[1],
        "offs": striped8(idx),
        "offs2": striped8(idx2),
        "offs3": striped8(idx3),
        "offs4": striped8(idx4),
        "offs5": striped8(idx5),
    }


def reference(query, keys_words, keys_scales, notes_words, notes_scales, users_words, users_scales, shelves_words, shelves_scales, offs, offs2, offs3, offs4, offs5):
    idx = unstriped8(offs)
    idx2 = unstriped8(offs2)
    idx3 = unstriped8(offs3)
    idx4 = unstriped8(offs4)
    idx5 = unstriped8(offs5)
    keysu = unpack_weight(keys_words, keys_scales, "e4m3")
    notesu = unpack_weight(notes_words, notes_scales, "e2m1")
    usersu = unpack_weight(users_words, users_scales, "e4m3")
    shelvesu = unpack_weight(shelves_words, shelves_scales, "e2m1")
    queryq = mxq(f64(query), 0, "e4m3")
    a = queryq.T @ keysu
    b = queryq.T @ notesu
    c0 = queryq.T @ usersu
    d0 = queryq.T @ shelvesu
    w = pick8(a, idx, 16) - pick8(b, idx2, 16)
    p2 = w.reshape(Q, J, I // J).sum(axis=2)
    v = np.maximum(p2, pick8(c0, idx3, 16))
    f1 = np.zeros((Q, S))
    f1[np.arange(Q)[:, None], idx4[np.arange(Q) % 128 // 16]] = v
    dd = d0 + f1
    y = pick8(dd, idx5, 16) - w
    return y

@@ -1,0 +1,166 @@
+from contextlib import ExitStack
+
+import concourse.mybir as mybir
+
+D, POOL, SLOTS, PAIRS, ROWS = 512, 1024, 512, 256, 128
+FLOPS = 4 * 2 * D * ROWS * POOL
+
+F32 = mybir.dt.float32
+BF16 = mybir.dt.bfloat16
+I32 = mybir.dt.int32
+U32 = mybir.dt.uint32
+U16 = mybir.dt.uint16
+U8 = mybir.dt.uint8
+FP8X4 = mybir.dt.float8_e4m3fn_x4
+FP4X4 = mybir.dt.float4_e2m1fn_x4
+ADD = mybir.AluOpType.add
+SUB = mybir.AluOpType.subtract
+MAX = mybir.AluOpType.max
+COPY = mybir.ActivationFunctionType.Copy
+
+P = 128
+PACK = 4
+BANK = 512
+HALF = SLOTS // 2
+
+
+def tile_attend_pairsoffour_four_kernel(
+    tc, query, keys_words, keys_scales, notes_words, notes_scales, users_words, users_scales,
+    shelves_words, shelves_scales, offs, offs2, offs3, offs4, offs5, out,
+):
+    nc = tc.nc
+    with ExitStack() as ctx:
+        sb = ctx.enter_context(tc.tile_pool(name="sb", bufs=1))
+        ps = ctx.enter_context(tc.psum_pool(name="ps", bufs=8))
+
+        def plane(name, engine):
+            tile = sb.tile([P, POOL], U8, name=name, tag=name, align_bytes=64)
+            engine.memset(tile[:].bitcast(U32), 0)
+            return tile
+
+        def load_plane_rows(queue, tile, scales, quadrants):
+            for quad in quadrants:
+                queue.dma_start(
+                    out=tile[32 * quad : 32 * quad + 4, :].bitcast(I32),
+                    in_=scales[0, 4 * quad : 4 * quad + 4, :].bitcast(I32),
+                )
+
+        def load_fp8_words(name, words):
+            tile = sb.tile([P, PACK * POOL], U8, name=name, align_bytes=64)
+            nc.sync.dma_start(
+                out=tile[:].bitcast(I32), in_=words[0].rearrange("p n t -> p (n t)").bitcast(I32)
+            )
+            return tile
+
+        def load_fp4_words(name, words):
+            tile = sb.tile([P, 2 * POOL], U8, name=name, align_bytes=64)
+            nc.sync.dma_start(out=tile[:].bitcast(I32), in_=words[0].bitcast(I32))
+            return tile
+
+        def load_list(name, lists):
+            tile = sb.tile(list(lists.shape), U16, name=name)
+            nc.sync.dma_start(tile[:], lists)
+            return tile
+
+        notes_plane = plane("notes_plane", nc.vector)
+        keys_plane = plane("keys_plane", nc.vector)
+        users_plane = plane("users_plane", nc.vector)
+        shelves_plane = plane("shelves_plane", nc.vector)
+        f1 = sb.tile([P, POOL], F32, name="f1")
+        nc.vector.memset(f1[:], 0.0)
+
+        q_raw = sb.tile([P, PACK, ROWS], F32, name="q_raw")
+        nc.sync.dma_start(out=q_raw[:], in_=query.rearrange("(p t) q -> p t q", t=PACK))
+        note_list = load_list("note_list", offs2)
+        load_plane_rows(nc.sync, notes_plane, notes_scales, range(2))
+        load_plane_rows(nc.scalar, notes_plane, notes_scales, range(2, 4))
+        notes_tile = load_fp4_words("notes_tile", notes_words)
+        keys_tile = load_fp8_words("keys_tile", keys_words)
+        load_plane_rows(nc.sync, keys_plane, keys_scales, range(4))
+        token_list = load_list("token_list", offs)
+        users_tile = load_fp8_words("users_tile", users_words)
+        load_plane_rows(nc.sync, users_plane, users_scales, range(4))
+        user_list = load_list("user_list", offs3)
+        put_list = load_list("put_list", offs4)
+        shelves_tile = load_fp4_words("shelves_tile", shelves_words)
+        load_plane_rows(nc.sync, shelves_plane, shelves_scales, range(4))
+        shelf_list = load_list("shelf_list", offs5)
+
+        q_bf = sb.tile([P, ROWS, PACK], BF16, name="q_bf", align_bytes=64)
+        nc.vector.tensor_copy(out=q_bf[:], in_=q_raw[:].rearrange("p t q -> p q t"))
+        q_codes = sb.tile([P, ROWS], U32, name="q_codes", align_bytes=64)
+        q_plane = sb.tile([P, ROWS], U8, name="q_plane", align_bytes=64)
+        nc.vector.quantize_mx(
+            out=q_codes[:].bitcast(FP8X4), scales=q_plane[:], in_=q_bf[:].rearrange("p q t -> p (q t)")
+        )
+
+        def product(words, word_bytes, dtype, scale_plane, lo, hi):
+            bank = ps.tile([P, hi - lo], F32, name="bank")
+            nc.tensor.matmul_mx(
+                out=bank[:],
+                lhsT=q_codes[:].bitcast(FP8X4),
+                lhsT_scale=q_plane[:],
+                rhs=words[:, word_bytes * lo : word_bytes * hi].bitcast(dtype),
+                rhs_scale=scale_plane[:, lo:hi],
+                start=True,
+                stop=True,
+            )
+            return bank
+
+        def on_vector(dst, src):
+            nc.vector.tensor_copy(dst, src)
+
+        def on_scalar(dst, src):
+            nc.scalar.activation(dst, src, COPY)
+
+        def scores(name, words, word_bytes, dtype, scale_plane, copies):
+            table = sb.tile([P, POOL], F32, name=name)
+            width = POOL // len(copies)
+            for piece, copy_out in enumerate(copies):
+                lo, hi = piece * width, (piece + 1) * width
+                copy_out(table[:, lo:hi], product(words, word_bytes, dtype, scale_plane, lo, hi)[:])
+            return table
+
+        halves = [slice(h * HALF, (h + 1) * HALF) for h in range(2)]
+        list_halves = [slice(h * HALF // 16, (h + 1) * HALF // 16) for h in range(2)]
+
+        b = scores("b", notes_tile, 2, FP4X4, notes_plane, [on_vector, on_scalar, on_vector, on_scalar])
+        a = scores("a", keys_tile, 4, FP8X4, keys_plane, [on_vector] * 4)
+        b_picked = sb.tile([P, SLOTS], F32, name="b_picked")
+        for h in range(2):
+            nc.scalar.activation(b_picked[:, halves[h]], b[:].indirect(note_list[:, list_halves[h]]), COPY)
+
+        def leads(h, tag):
+            w_half = sb.tile([P, HALF], F32, name=f"w{h}", tag=tag, align_bytes=64)
+            nc.vector.tensor_tensor(
+                w_half[:], a[:].indirect(token_list[:, list_halves[h]]), b_picked[:, halves[h]], SUB
+            )
+            return w_half
+
+        w = [leads(0, "w0")]
+        c0 = scores("c0", users_tile, 4, FP8X4, users_plane, [on_scalar, on_vector, on_scalar, on_vector])
+        w.append(leads(1, "users_plane"))
+        c_picked = sb.tile([P, PAIRS], F32, name="c_picked")
+        nc.scalar.activation(c_picked[:], c0[:].indirect(user_list[:]), COPY)
+
+        p2 = sb.tile([P, PAIRS], F32, name="p2")
+        v = sb.tile([P, PAIRS], F32, name="v")
+        pair_halves = [slice(h * PAIRS // 2, (h + 1) * PAIRS // 2) for h in range(2)]
+        for h in range(2):
+            nc.vector.tensor_tensor(p2[:, pair_halves[h]], w[h][:, 0:HALF:2], w[h][:, 1:HALF:2], ADD)
+        for h in range(2):
+            nc.vector.tensor_tensor(v[:, pair_halves[h]], p2[:, pair_halves[h]], c_picked[:, pair_halves[h]], MAX)
+        nc.vector.tensor_copy(f1[:].indirect(put_list[:]), v[:])
+
+        dd = sb.tile([P, POOL], F32, name="dd")
+        for lo in range(0, POOL, BANK):
+            d_bank = product(shelves_tile, 2, FP4X4, shelves_plane, lo, lo + BANK)
+            nc.vector.tensor_tensor(dd[:, lo : lo + BANK], d_bank[:], f1[:, lo : lo + BANK], ADD)
+
+        y = [sb.tile([P, HALF], F32, name=f"y{h}") for h in range(2)]
+        dd_picked = sb.tile([P, HALF], F32, name="dd_picked")
+        nc.scalar.activation(dd_picked[:], dd[:].indirect(shelf_list[:, list_halves[1]]), COPY)
+        nc.vector.tensor_tensor(y[0][:], dd[:].indirect(shelf_list[:, list_halves[0]]), w[0][:], SUB)
+        nc.sync.dma_start(out=out[:, halves[0]], in_=y[0][:])
+        nc.vector.tensor_tensor(y[1][:], dd_picked[:], w[1][:], SUB)
+        nc.scalar.dma_start(out=out[:, halves[1]], in_=y[1][:])

@@ -38,11 +38,11 @@ def tile_attend_pairsoffour_four_kernel(
             engine.memset(tile[:].bitcast(U32), 0)
             return tile
 
-        def load_plane_rows(queue, tile, scales, quadrants):
-            for quad in quadrants:
+        def load_plane_rows(queue, tile, first, scales, rows):
+            for row in rows:
                 queue.dma_start(
-                    out=tile[32 * quad : 32 * quad + 4, :].bitcast(I32),
-                    in_=scales[0, 4 * quad : 4 * quad + 4, :].bitcast(I32),
+                    out=tile[first + row : P : 32, :].bitcast(I32),
+                    in_=scales[0, row:16:4, :].bitcast(I32),
                 )
 
         def load_fp8_words(name, words):
@@ -72,18 +72,18 @@ def tile_attend_pairsoffour_four_kernel(
         q_raw = sb.tile([P, PACK, ROWS], F32, name="q_raw")
         nc.sync.dma_start(out=q_raw[:], in_=query.rearrange("(p t) q -> p t q", t=PACK))
         note_list = load_list("note_list", offs2)
-        load_plane_rows(nc.sync, notes_plane, notes_scales, range(2))
-        load_plane_rows(nc.scalar, notes_plane, notes_scales, range(2, 4))
+        load_plane_rows(nc.sync, notes_plane, 0, notes_scales, range(2))
+        load_plane_rows(nc.scalar, notes_plane, 0, notes_scales, range(2, 4))
         notes_tile = load_fp4_words("notes_tile", notes_words)
         keys_tile = load_fp8_words("keys_tile", keys_words)
-        load_plane_rows(nc.sync, keys_plane, keys_scales, range(4))
+        load_plane_rows(nc.sync, keys_plane, 4, keys_scales, range(4))
         token_list = load_list("token_list", offs)
         users_tile = load_fp8_words("users_tile", users_words)
-        load_plane_rows(nc.sync, users_plane, users_scales, range(4))
+        load_plane_rows(nc.sync, users_plane, 8, users_scales, range(4))
         user_list = load_list("user_list", offs3)
         put_list = load_list("put_list", offs4)
         shelves_tile = load_fp4_words("shelves_tile", shelves_words)
-        load_plane_rows(nc.sync, shelves_plane, shelves_scales, range(4))
+        load_plane_rows(nc.sync, shelves_plane, 0, shelves_scales, range(4))
         shelf_list = load_list("shelf_list", offs5)
 
         q_bf = sb.tile([P, ROWS, PACK], BF16, name="q_bf", align_bytes=64)
@@ -124,8 +124,8 @@ def tile_attend_pairsoffour_four_kernel(
         halves = [slice(h * HALF, (h + 1) * HALF) for h in range(2)]
         list_halves = [slice(h * HALF // 16, (h + 1) * HALF // 16) for h in range(2)]
 
-        b = scores("b", notes_tile, 2, FP4X4, notes_plane, [on_vector, on_scalar, on_vector, on_scalar])
-        a = scores("a", keys_tile, 4, FP8X4, keys_plane, [on_vector] * 4)
+        b = scores("b", notes_tile, 2, FP4X4, notes_plane[:], [on_vector, on_scalar, on_vector, on_scalar])
+        a = scores("a", keys_tile, 4, FP8X4, keys_plane[4:P, :], [on_vector] * 4)
         b_picked = sb.tile([P, SLOTS], F32, name="b_picked")
         for h in range(2):
             nc.scalar.activation(b_picked[:, halves[h]], b[:].indirect(note_list[:, list_halves[h]]), COPY)
@@ -138,7 +138,7 @@ def tile_attend_pairsoffour_four_kernel(
             return w_half
 
         w = [leads(0, "w0")]
-        c0 = scores("c0", users_tile, 4, FP8X4, users_plane, [on_scalar, on_vector, on_scalar, on_vector])
+        c0 = scores("c0", users_tile, 4, FP8X4, users_plane[8:P, :], [on_scalar, on_vector, on_scalar, on_vector])
         w.append(leads(1, "users_plane"))
         c_picked = sb.tile([P, PAIRS], F32, name="c_picked")
         nc.scalar.activation(c_picked[:], c0[:].indirect(user_list[:]), COPY)
@@ -153,9 +153,13 @@ def tile_attend_pairsoffour_four_kernel(
         nc.vector.tensor_copy(f1[:].indirect(put_list[:]), v[:])
 
         dd = sb.tile([P, POOL], F32, name="dd")
-        for lo in range(0, POOL, BANK):
-            d_bank = product(shelves_tile, 2, FP4X4, shelves_plane, lo, lo + BANK)
-            nc.vector.tensor_tensor(dd[:, lo : lo + BANK], d_bank[:], f1[:, lo : lo + BANK], ADD)
+        split = 3 * POOL // 4
+        d_tail = sb.tile([P, POOL - split], F32, name="d_tail")
+        on_scalar(d_tail[:], product(shelves_tile, 2, FP4X4, shelves_plane[:], split, POOL)[:])
+        nc.gpsimd.tensor_tensor(dd[:, split:], d_tail[:], f1[:, split:], ADD)
+        for lo, hi in ((0, BANK), (BANK, split)):
+            d_bank = product(shelves_tile, 2, FP4X4, shelves_plane[:], lo, hi)
+            nc.vector.tensor_tensor(dd[:, lo:hi], d_bank[:], f1[:, lo:hi], ADD)
 
         y = [sb.tile([P, HALF], F32, name=f"y{h}") for h in range(2)]
         dd_picked = sb.tile([P, HALF], F32, name="dd_picked")

@@ -66,8 +66,6 @@ def tile_attend_pairsoffour_four_kernel(
         keys_plane = plane("keys_plane", nc.vector)
         users_plane = plane("users_plane", nc.vector)
         shelves_plane = plane("shelves_plane", nc.vector)
-        f1 = sb.tile([P, POOL], F32, name="f1")
-        nc.vector.memset(f1[:], 0.0)
 
         q_raw = sb.tile([P, PACK, ROWS], F32, name="q_raw")
         nc.sync.dma_start(out=q_raw[:], in_=query.rearrange("(p t) q -> p t q", t=PACK))
@@ -77,22 +75,26 @@ def tile_attend_pairsoffour_four_kernel(
         notes_tile = load_fp4_words("notes_tile", notes_words)
         keys_tile = load_fp8_words("keys_tile", keys_words)
         load_plane_rows(nc.sync, keys_plane, 4, keys_scales, range(4))
-        token_list = load_list("token_list", offs)
         users_tile = load_fp8_words("users_tile", users_words)
-        load_plane_rows(nc.sync, users_plane, 8, users_scales, range(4))
+        load_plane_rows(nc.sync, users_plane, 8, users_scales, range(2))
+        load_plane_rows(nc.gpsimd, users_plane, 8, users_scales, range(2, 4))
+        token_list = load_list("token_list", offs)
         user_list = load_list("user_list", offs3)
         put_list = load_list("put_list", offs4)
         shelves_tile = load_fp4_words("shelves_tile", shelves_words)
         load_plane_rows(nc.sync, shelves_plane, 0, shelves_scales, range(4))
         shelf_list = load_list("shelf_list", offs5)
 
-        q_bf = sb.tile([P, ROWS, PACK], BF16, name="q_bf", align_bytes=64)
+        q_bf = sb.tile([P, ROWS, PACK], BF16, name="q_bf", tag="q_bf", align_bytes=64)
         nc.vector.tensor_copy(out=q_bf[:], in_=q_raw[:].rearrange("p t q -> p q t"))
         q_codes = sb.tile([P, ROWS], U32, name="q_codes", align_bytes=64)
         q_plane = sb.tile([P, ROWS], U8, name="q_plane", align_bytes=64)
         nc.vector.quantize_mx(
             out=q_codes[:].bitcast(FP8X4), scales=q_plane[:], in_=q_bf[:].rearrange("p q t -> p (q t)")
         )
+
+        f1 = sb.tile([P, POOL], F32, name="f1", tag="q_bf", align_bytes=64)
+        nc.gpsimd.memset(f1[:], 0.0)
 
         def product(words, word_bytes, dtype, scale_plane, lo, hi):
             bank = ps.tile([P, hi - lo], F32, name="bank")
@@ -130,16 +132,15 @@ def tile_attend_pairsoffour_four_kernel(
         for h in range(2):
             nc.scalar.activation(b_picked[:, halves[h]], b[:].indirect(note_list[:, list_halves[h]]), COPY)
 
-        def leads(h, tag):
-            w_half = sb.tile([P, HALF], F32, name=f"w{h}", tag=tag, align_bytes=64)
+        def leads(h):
+            w_half = sb.tile([P, HALF], F32, name=f"w{h}")
             nc.vector.tensor_tensor(
                 w_half[:], a[:].indirect(token_list[:, list_halves[h]]), b_picked[:, halves[h]], SUB
             )
             return w_half
 
-        w = [leads(0, "w0")]
-        c0 = scores("c0", users_tile, 4, FP8X4, users_plane[8:P, :], [on_scalar, on_vector, on_scalar, on_vector])
-        w.append(leads(1, "users_plane"))
+        c0 = scores("c0", users_tile, 4, FP8X4, users_plane[8:P, :], [on_vector, on_scalar, on_scalar, on_scalar])
+        w = [leads(h) for h in range(2)]
         c_picked = sb.tile([P, PAIRS], F32, name="c_picked")
         nc.scalar.activation(c_picked[:], c0[:].indirect(user_list[:]), COPY)
 

@@ -162,10 +162,7 @@ def tile_attend_pairsoffour_four_kernel(
             d_bank = product(shelves_tile, 2, FP4X4, shelves_plane[:], lo, hi)
             nc.vector.tensor_tensor(dd[:, lo:hi], d_bank[:], f1[:, lo:hi], ADD)
 
-        y = [sb.tile([P, HALF], F32, name=f"y{h}") for h in range(2)]
-        dd_picked = sb.tile([P, HALF], F32, name="dd_picked")
-        nc.scalar.activation(dd_picked[:], dd[:].indirect(shelf_list[:, list_halves[1]]), COPY)
-        nc.vector.tensor_tensor(y[0][:], dd[:].indirect(shelf_list[:, list_halves[0]]), w[0][:], SUB)
-        nc.sync.dma_start(out=out[:, halves[0]], in_=y[0][:])
-        nc.vector.tensor_tensor(y[1][:], dd_picked[:], w[1][:], SUB)
-        nc.scalar.dma_start(out=out[:, halves[1]], in_=y[1][:])
+        for h, queue in enumerate((nc.sync, nc.scalar)):
+            y = sb.tile([P, HALF], F32, name=f"y{h}")
+            nc.vector.tensor_tensor(y[:], dd[:].indirect(shelf_list[:, list_halves[h]]), w[h][:], SUB)
+            queue.dma_start(out=out[:, halves[h]], in_=y[:])

from contextlib import ExitStack

import concourse.mybir as mybir

D, POOL, SLOTS, PAIRS, ROWS = 512, 1024, 512, 256, 128
FLOPS = 4 * 2 * D * ROWS * POOL

F32 = mybir.dt.float32
BF16 = mybir.dt.bfloat16
I32 = mybir.dt.int32
U32 = mybir.dt.uint32
U16 = mybir.dt.uint16
U8 = mybir.dt.uint8
FP8X4 = mybir.dt.float8_e4m3fn_x4
FP4X4 = mybir.dt.float4_e2m1fn_x4
ADD = mybir.AluOpType.add
SUB = mybir.AluOpType.subtract
MAX = mybir.AluOpType.max
COPY = mybir.ActivationFunctionType.Copy

P = 128
PACK = 4
BANK = 512
HALF = SLOTS // 2


def tile_attend_pairsoffour_four_kernel(
    tc, query, keys_words, keys_scales, notes_words, notes_scales, users_words, users_scales,
    shelves_words, shelves_scales, offs, offs2, offs3, offs4, offs5, out,
):
    nc = tc.nc
    with ExitStack() as ctx:
        sb = ctx.enter_context(tc.tile_pool(name="sb", bufs=1))
        ps = ctx.enter_context(tc.psum_pool(name="ps", bufs=8))

        def plane(name, engine):
            tile = sb.tile([P, POOL], U8, name=name, tag=name, align_bytes=64)
            engine.memset(tile[:].bitcast(U32), 0)
            return tile

        def load_plane_rows(queue, tile, first, scales, rows):
            for row in rows:
                queue.dma_start(
                    out=tile[first + row : P : 32, :].bitcast(I32),
                    in_=scales[0, row:16:4, :].bitcast(I32),
                )

        def load_fp8_words(name, words):
            tile = sb.tile([P, PACK * POOL], U8, name=name, align_bytes=64)
            nc.sync.dma_start(
                out=tile[:].bitcast(I32), in_=words[0].rearrange("p n t -> p (n t)").bitcast(I32)
            )
            return tile

        def load_fp4_words(name, words):
            tile = sb.tile([P, 2 * POOL], U8, name=name, align_bytes=64)
            nc.sync.dma_start(out=tile[:].bitcast(I32), in_=words[0].bitcast(I32))
            return tile

        def load_list(name, lists):
            tile = sb.tile(list(lists.shape), U16, name=name)
            nc.sync.dma_start(tile[:], lists)
            return tile

        notes_plane = plane("notes_plane", nc.vector)
        keys_plane = plane("keys_plane", nc.vector)
        users_plane = plane("users_plane", nc.vector)
        shelves_plane = plane("shelves_plane", nc.vector)

        q_raw = sb.tile([P, PACK, ROWS], F32, name="q_raw")
        nc.sync.dma_start(out=q_raw[:], in_=query.rearrange("(p t) q -> p t q", t=PACK))
        note_list = load_list("note_list", offs2)
        load_plane_rows(nc.sync, notes_plane, 0, notes_scales, range(2))
        load_plane_rows(nc.scalar, notes_plane, 0, notes_scales, range(2, 4))
        notes_tile = load_fp4_words("notes_tile", notes_words)
        keys_tile = load_fp8_words("keys_tile", keys_words)
        load_plane_rows(nc.sync, keys_plane, 4, keys_scales, range(4))
        users_tile = load_fp8_words("users_tile", users_words)
        load_plane_rows(nc.sync, users_plane, 8, users_scales, range(2))
        load_plane_rows(nc.gpsimd, users_plane, 8, users_scales, range(2, 4))
        token_list = load_list("token_list", offs)
        user_list = load_list("user_list", offs3)
        put_list = load_list("put_list", offs4)
        shelves_tile = load_fp4_words("shelves_tile", shelves_words)
        load_plane_rows(nc.sync, shelves_plane, 0, shelves_scales, range(4))
        shelf_list = load_list("shelf_list", offs5)

        q_bf = sb.tile([P, ROWS, PACK], BF16, name="q_bf", tag="q_bf", align_bytes=64)
        nc.vector.tensor_copy(out=q_bf[:], in_=q_raw[:].rearrange("p t q -> p q t"))
        q_codes = sb.tile([P, ROWS], U32, name="q_codes", align_bytes=64)
        q_plane = sb.tile([P, ROWS], U8, name="q_plane", align_bytes=64)
        nc.vector.quantize_mx(
            out=q_codes[:].bitcast(FP8X4), scales=q_plane[:], in_=q_bf[:].rearrange("p q t -> p (q t)")
        )

        f1 = sb.tile([P, POOL], F32, name="f1", tag="q_bf", align_bytes=64)
        nc.gpsimd.memset(f1[:], 0.0)

        def product(words, word_bytes, dtype, scale_plane, lo, hi):
            bank = ps.tile([P, hi - lo], F32, name="bank")
            nc.tensor.matmul_mx(
                out=bank[:],
                lhsT=q_codes[:].bitcast(FP8X4),
                lhsT_scale=q_plane[:],
                rhs=words[:, word_bytes * lo : word_bytes * hi].bitcast(dtype),
                rhs_scale=scale_plane[:, lo:hi],
                start=True,
                stop=True,
            )
            return bank

        def on_vector(dst, src):
            nc.vector.tensor_copy(dst, src)

        def on_scalar(dst, src):
            nc.scalar.activation(dst, src, COPY)

        def scores(name, words, word_bytes, dtype, scale_plane, copies):
            table = sb.tile([P, POOL], F32, name=name)
            width = POOL // len(copies)
            for piece, copy_out in enumerate(copies):
                lo, hi = piece * width, (piece + 1) * width
                copy_out(table[:, lo:hi], product(words, word_bytes, dtype, scale_plane, lo, hi)[:])
            return table

        halves = [slice(h * HALF, (h + 1) * HALF) for h in range(2)]
        list_halves = [slice(h * HALF // 16, (h + 1) * HALF // 16) for h in range(2)]

        b = scores("b", notes_tile, 2, FP4X4, notes_plane[:], [on_vector, on_scalar, on_vector, on_scalar])
        a = scores("a", keys_tile, 4, FP8X4, keys_plane[4:P, :], [on_vector] * 4)
        b_picked = sb.tile([P, SLOTS], F32, name="b_picked")
        for h in range(2):
            nc.scalar.activation(b_picked[:, halves[h]], b[:].indirect(note_list[:, list_halves[h]]), COPY)

        def leads(h):
            w_half = sb.tile([P, HALF], F32, name=f"w{h}")
            nc.vector.tensor_tensor(
                w_half[:], a[:].indirect(token_list[:, list_halves[h]]), b_picked[:, halves[h]], SUB
            )
            return w_half

        c0 = scores("c0", users_tile, 4, FP8X4, users_plane[8:P, :], [on_vector, on_scalar, on_scalar, on_scalar])
        w = [leads(h) for h in range(2)]
        c_picked = sb.tile([P, PAIRS], F32, name="c_picked")
        nc.scalar.activation(c_picked[:], c0[:].indirect(user_list[:]), COPY)

        p2 = sb.tile([P, PAIRS], F32, name="p2")
        v = sb.tile([P, PAIRS], F32, name="v")
        pair_halves = [slice(h * PAIRS // 2, (h + 1) * PAIRS // 2) for h in range(2)]
        for h in range(2):
            nc.vector.tensor_tensor(p2[:, pair_halves[h]], w[h][:, 0:HALF:2], w[h][:, 1:HALF:2], ADD)
        for h in range(2):
            nc.vector.tensor_tensor(v[:, pair_halves[h]], p2[:, pair_halves[h]], c_picked[:, pair_halves[h]], MAX)
        nc.vector.tensor_copy(f1[:].indirect(put_list[:]), v[:])

        dd = sb.tile([P, POOL], F32, name="dd")
        split = 3 * POOL // 4
        d_tail = sb.tile([P, POOL - split], F32, name="d_tail")
        on_scalar(d_tail[:], product(shelves_tile, 2, FP4X4, shelves_plane[:], split, POOL)[:])
        nc.gpsimd.tensor_tensor(dd[:, split:], d_tail[:], f1[:, split:], ADD)
        for lo, hi in ((0, BANK), (BANK, split)):
            d_bank = product(shelves_tile, 2, FP4X4, shelves_plane[:], lo, hi)
            nc.vector.tensor_tensor(dd[:, lo:hi], d_bank[:], f1[:, lo:hi], ADD)

        for h, queue in enumerate((nc.sync, nc.scalar)):
            y = sb.tile([P, HALF], F32, name=f"y{h}")
            nc.vector.tensor_tensor(y[:], dd[:].indirect(shelf_list[:, list_halves[h]]), w[h][:], SUB)
            queue.dma_start(out=out[:, halves[h]], in_=y[:])
